import numpy as np
import ml_dtypes


def mxq(x, axis, fmt="e4m3"):
    dtype, down = {"e4m3": (ml_dtypes.float8_e4m3fn, 7), "e5m2": (ml_dtypes.float8_e5m2, 14)}[fmt]
    v = np.moveaxis(np.asarray(x, np.float32).astype(ml_dtypes.bfloat16).astype(np.float64), axis, -1)
    blocks = v.reshape(v.shape[:-1] + (-1, 32))
    amax = np.abs(blocks).max(-1, keepdims=True)
    byte = np.maximum(np.where(amax > 0, np.frexp(amax)[1] - 1 + 127, 0) - down, 1)
    scale = np.exp2(byte - 127.0)
    codes = (blocks / scale).astype(np.float32).astype(dtype).astype(np.float64)
    return np.moveaxis((codes * scale).reshape(v.shape), -1, axis)


WIDE = False


def mx_kscale(k):
    if not WIDE:
        return np.ones(k)
    levels = np.array([18, -18])
    if k % 512:
        return np.exp2(np.random.permutation(np.resize(levels, k // 32))).repeat(32)
    a = np.empty((k // 512, 16))
    for p in range(k // 512):
        a[p, :8] = np.random.permutation(np.resize(levels, 8))
        for g in range(8):
            far = levels[np.abs(levels - a[p, g]) >= 10]
            a[p, g + 8] = far[np.random.randint(len(far))]
    return np.exp2(a.ravel()).repeat(32)


def f64(x):
    return np.asarray(x).astype(np.float64)


def striped(idx):
    return np.tile(np.asarray(idx).reshape(-1, 16).T, (8, 1)).astype(np.uint16)


def unstriped(offs):
    return offs[:16].T.reshape(-1).astype(np.int64)


E2M1 = np.array([0.0, 0.5, 1.0, 1.5, 2.0, 3.0, 4.0, 6.0, -0.0, -0.5, -1.0, -1.5, -2.0, -3.0, -4.0, -6.0])


def pack_weight(w, fmt):
    k, n = w.shape
    w = f64(np.asarray(w, np.float32).astype(ml_dtypes.bfloat16)).reshape(k // 32, 32, n)
    amax = np.abs(w).max(1)
    if fmt == "e4m3":
        byte = np.frexp(amax)[1] - 1 + 127 - 7
    else:
        mant, ex = np.frexp(amax / 6.0)
        byte = np.where(mant > 0.5, ex, ex - 1) + 127
    byte = np.clip(np.where(amax > 0, byte, 1), 1, 254)
    scaled = (w * np.exp2(127.0 - byte)[:, None, :]).reshape(k, n).astype(np.float32)
    by_word = np.ascontiguousarray(scaled.reshape(k // 512, 128, 4, n).transpose(0, 1, 3, 2))
    if fmt == "e4m3":
        words = by_word.astype(ml_dtypes.float8_e4m3fn).view(np.uint8)
    else:
        c = by_word.astype(ml_dtypes.float4_e2m1fn).view(np.uint8) & 0xF
        words = (c[..., 0::2] | (c[..., 1::2] << 4)).reshape(k // 512, 128, 2 * n)
    return np.ascontiguousarray(words), np.ascontiguousarray(byte.astype(np.uint8).reshape(k // 512, 16, n))


def unpack_weight(words, scales, fmt):
    g, _, n = scales.shape
    words = np.ascontiguousarray(words).reshape(g, 128, n, -1)
    if fmt == "e4m3":
        vals = words.view(ml_dtypes.float8_e4m3fn).astype(np.float64)
    else:
        nib = np.empty((g, 128, n, 4), np.uint8)
        nib[..., 0::2] = words & 0xF
        nib[..., 1::2] = words >> 4
        vals = E2M1[nib]
    vals = vals * np.repeat(np.exp2(scales.astype(np.float64) - 127.0), 8, axis=1)[..., None]
    return vals.transpose(0, 1, 3, 2).reshape(g * 512, n)


V, K, E, D, DV = 1024, 2, 2048, 512, 512


def setup_inputs():
    n = np.random.standard_normal
    v = mx_kscale(DV)[:, None]
    coarse = lambda x: x.astype(np.float32).astype(ml_dtypes.bfloat16).astype(np.float64)
    wp = pack_weight(n((DV, D)) / np.sqrt(DV) / v, "e2m1")
    return {
        "dyT": (coarse(n((DV, V))) * v).astype(np.float32),
        "hE": (np.random.randint(1, 32, (DV, E)) / 32.0).astype(np.float32),
        "ew": np.tile(np.random.randint(8, 33, E) / 16.0, (128, 1)).astype(np.float32),
        "w_words": wp[0],
        "w_scales": wp[1],
        "offs": striped(np.random.randint(0, V, E)),
        "offs2": striped(np.random.permutation(E)),
    }


def reference(dyT, hE, ew, w_words, w_scales, offs, offs2):
    h = f64(hE)
    dz = f64(ew)[:1] * f64(dyT)[:, unstriped(offs)] * h * (1.0 - h)
    dm = unpack_weight(w_words, w_scales, "e2m1").T @ mxq(dz, 0, "e5m2")
    return dm[:, unstriped(offs2)].reshape(D, V, K).sum(-1)

@@ -1,0 +1,163 @@
+from contextlib import ExitStack
+
+import concourse.mybir as mybir
+
+F32 = mybir.dt.float32
+BF16 = mybir.dt.bfloat16
+U32 = mybir.dt.uint32
+I32 = mybir.dt.int32
+U16 = mybir.dt.uint16
+U8 = mybir.dt.uint8
+E5M2X4 = mybir.dt.float8_e5m2_x4
+E2M1X4 = mybir.dt.float4_e2m1fn_x4
+ALU = mybir.AluOpType
+ACT = mybir.ActivationFunctionType
+
+P = 128
+V, E, D, DV = 1024, 2048, 512, 512
+PACK = 4
+CHUNK = 512
+NCHUNK = E // CHUNK
+NBLK = D // P
+PIECE = 1024
+
+FLOPS = 2 * DV * D * E
+
+
+def tile_attend_gmp_sig_ew_kernel(tc, dyT, hE, ew, w_words, w_scales, offs, offs2, out):
+    nc = tc.nc
+    with ExitStack() as ctx:
+        keep = ctx.enter_context(tc.tile_pool(name="keep", bufs=1))
+        ring = ctx.enter_context(tc.tile_pool(name="ring", bufs=2))
+        psum = ctx.enter_context(tc.psum_pool(name="psum", bufs=1))
+
+        dst = keep.tile([P, E // 16], U16, name="dst")
+        src = keep.tile([P, E // 16], U16, name="src")
+        dy = [keep.tile([P, V], F32, name="dy%d" % t) for t in range(PACK)]
+        ewc = [keep.tile([P, CHUNK], F32, name="ew%d" % c) for c in range(NCHUNK)]
+        h = [keep.tile([P, PACK, CHUNK], F32, name="h%d" % c) for c in range(NCHUNK)]
+        g = [keep.tile([P, PACK, CHUNK], F32, name="g%d" % c) for c in range(NCHUNK)]
+        words = keep.tile([P, 2 * D], U8, name="words", align_bytes=64)
+        wsc = keep.tile([P, D], U8, name="wsc", align_bytes=64)
+        codes = [keep.tile([P, CHUNK], U32, name="codes%d" % c, align_bytes=64) for c in range(NCHUNK)]
+        scales = [keep.tile([P, CHUNK], U8, name="scales%d" % c, align_bytes=64) for c in range(NCHUNK)]
+        dm = [keep.tile([P, E], F32, name="dm%d" % b) for b in range(NBLK)]
+
+        dy_planes = dyT.rearrange("(p t) v -> p t v", t=PACK)
+        h_planes = hE.rearrange("(p t) e -> p t e", t=PACK)
+
+        def cols(c):
+            return slice(c * CHUNK, (c + 1) * CHUNK)
+
+        nc.gpsimd.memset(wsc[:].bitcast(I32), 0)
+        nc.sync.dma_start(dst[:], offs)
+        nc.sync.dma_start(ewc[0][:], ew[:, cols(0)])
+        nc.sync.dma_start(dy[0][:], dy_planes[:, 0, :])
+        nc.sync.dma_start(ewc[1][:], ew[:, cols(1)])
+        nc.sync.dma_start(dy[1][:], dy_planes[:, 1, :])
+        nc.sync.dma_start(dy[2][:], dy_planes[:, 2, :])
+        nc.sync.dma_start(h[0][:], h_planes[:, :, cols(0)])
+        nc.sync.dma_start(dy[3][:], dy_planes[:, 3, :])
+        nc.sync.dma_start(h[1][:], h_planes[:, :, cols(1)])
+        nc.sync.dma_start(ewc[2][:], ew[:, cols(2)])
+        nc.sync.dma_start(ewc[3][:], ew[:, cols(3)])
+        nc.sync.dma_start(h[2][:], h_planes[:, :, cols(2)])
+        nc.sync.dma_start(words[:].bitcast(I32), w_words[0].bitcast(I32))
+        for q in range(4):
+            nc.sync.dma_start(
+                wsc[32 * q : 32 * q + 4, :].bitcast(I32), w_scales[0, 4 * q : 4 * q + 4, :].bitcast(I32)
+            )
+        nc.sync.dma_start(h[3][:], h_planes[:, :, cols(3)])
+        nc.sync.dma_start(src[:], offs2)
+
+        def gather_dy(c, t):
+            k = CHUNK // 16
+            nc.vector.tensor_tensor(
+                g[c][:, t, :], dy[t][:].indirect(dst[:, c * k : (c + 1) * k]), ewc[c][:], ALU.mult
+            )
+
+        sq = {}
+        dz = {}
+
+        def square(c):
+            sq[c] = ring.tile([P, CHUNK, PACK], F32, name="sq")
+            nc.scalar.activation(
+                sq[c][:].rearrange("p (c i) t -> p c t i", i=2),
+                h[c][:].rearrange("p t (c i) -> p c t i", i=2),
+                ACT.Square,
+                bias=-0.5,
+            )
+
+        def form_dz(c):
+            dz[c] = ring.tile([P, CHUNK, PACK], BF16, name="dz", align_bytes=64)
+            nc.vector.scalar_tensor_tensor(
+                dz[c][:], sq[c][:], 0.25, g[c][:].rearrange("p t e -> p e t"), ALU.subtract, ALU.mult
+            )
+
+        def quantise(c):
+            nc.vector.quantize_mx(
+                out=codes[c][:].bitcast(E5M2X4), scales=scales[c][:], in_=dz[c][:].rearrange("p e t -> p (e t)")
+            )
+
+        def product(b, c):
+            if b == 0:
+                acc = psum.tile([P, CHUNK], F32, name="acc_first", bufs=2)
+            else:
+                acc = psum.tile([P, CHUNK], F32, name="acc", bufs=3)
+            nc.tensor.matmul_mx(
+                out=acc[:],
+                lhsT=words[:, 2 * P * b : 2 * P * (b + 1)].bitcast(E2M1X4),
+                lhsT_scale=wsc[:, P * b : P * (b + 1)],
+                rhs=codes[c][:].bitcast(E5M2X4),
+                rhs_scale=scales[c][:],
+                start=True,
+                stop=True,
+            )
+            nc.scalar.activation(dm[b][:, cols(c)], acc[:], ACT.Copy, scale=-1.0)
+
+        for t in range(PACK):
+            gather_dy(0, t)
+            gather_dy(1, t)
+        square(0)
+        square(1)
+        form_dz(0)
+        gather_dy(2, 0)
+        quantise(0)
+        product(0, 0)
+        form_dz(1)
+        gather_dy(2, 1)
+        quantise(1)
+        product(0, 1)
+        square(2)
+        gather_dy(2, 2)
+        gather_dy(2, 3)
+        form_dz(2)
+        gather_dy(3, 0)
+        quantise(2)
+        product(0, 2)
+        square(3)
+        for t in range(1, PACK):
+            gather_dy(3, t)
+        form_dz(3)
+        quantise(3)
+        product(0, 3)
+        for b in range(1, NBLK):
+            for c in range(NCHUNK):
+                product(b, c)
+
+        pending = []
+
+        def pair_sum(b, s, pairs):
+            res = ring.tile([P, PIECE // 2], F32, name="res", bufs=3)
+            nc.vector.tensor_tensor(res[:], pairs[:, 0:PIECE:2], pairs[:, 1:PIECE:2], ALU.add)
+            nc.sync.dma_start(out[P * b : P * (b + 1), s * (PIECE // 2) : (s + 1) * (PIECE // 2)], res[:])
+
+        for b in range(NBLK):
+            for s in range(E // PIECE):
+                k = PIECE // 16
+                pairs = ring.tile([P, PIECE], F32, name="pairs", bufs=3)
+                nc.vector.tensor_copy(pairs[:], dm[b][:].indirect(src[:, s * k : (s + 1) * k]))
+                if pending:
+                    pair_sum(*pending.pop())
+                pending.append((b, s, pairs))
+        pair_sum(*pending.pop())

@@ -80,18 +80,18 @@ def tile_attend_gmp_sig_ew_kernel(tc, dyT, hE, ew, w_words, w_scales, offs, offs
         dz = {}
 
         def square(c):
-            sq[c] = ring.tile([P, CHUNK, PACK], F32, name="sq")
-            nc.scalar.activation(
-                sq[c][:].rearrange("p (c i) t -> p c t i", i=2),
-                h[c][:].rearrange("p t (c i) -> p c t i", i=2),
-                ACT.Square,
-                bias=-0.5,
-            )
+            half = ring.tile([P, PACK, CHUNK], F32, name="half")
+            sq[c] = ring.tile([P, PACK, CHUNK], F32, name="sq")
+            nc.scalar.activation(half[:], h[c][:], ACT.Square, bias=-0.5)
+            nc.scalar.activation(sq[c][:], half[:], ACT.Copy, scale=-1.0, bias=0.25)
 
         def form_dz(c):
             dz[c] = ring.tile([P, CHUNK, PACK], BF16, name="dz", align_bytes=64)
-            nc.vector.scalar_tensor_tensor(
-                dz[c][:], sq[c][:], 0.25, g[c][:].rearrange("p t e -> p e t"), ALU.subtract, ALU.mult
+            nc.vector.tensor_tensor(
+                dz[c][:].rearrange("p (c i) t -> p c t i", i=2),
+                g[c][:].rearrange("p t (c i) -> p c t i", i=2),
+                sq[c][:].rearrange("p t (c i) -> p c t i", i=2),
+                ALU.mult,
             )
 
         def quantise(c):
@@ -103,7 +103,7 @@ def tile_attend_gmp_sig_ew_kernel(tc, dyT, hE, ew, w_words, w_scales, offs, offs
             if b == 0:
                 acc = psum.tile([P, CHUNK], F32, name="acc_first", bufs=2)
             else:
-                acc = psum.tile([P, CHUNK], F32, name="acc", bufs=3)
+                acc = psum.tile([P, CHUNK], F32, name="acc", bufs=4)
             nc.tensor.matmul_mx(
                 out=acc[:],
                 lhsT=words[:, 2 * P * b : 2 * P * (b + 1)].bitcast(E2M1X4),
@@ -113,7 +113,7 @@ def tile_attend_gmp_sig_ew_kernel(tc, dyT, hE, ew, w_words, w_scales, offs, offs
                 start=True,
                 stop=True,
             )
-            nc.scalar.activation(dm[b][:, cols(c)], acc[:], ACT.Copy, scale=-1.0)
+            nc.scalar.copy(dm[b][:, cols(c)], acc[:])
 
         for t in range(PACK):
             gather_dy(0, t)
@@ -145,19 +145,31 @@ def tile_attend_gmp_sig_ew_kernel(tc, dyT, hE, ew, w_words, w_scales, offs, offs
             for c in range(NCHUNK):
                 product(b, c)
 
+        def rows(b):
+            return slice(P * b, P * (b + 1))
+
+        def sum_on_vector(b, first, n, pairs):
+            res = ring.tile([P, n // 2], F32, name="res_v", bufs=2)
+            nc.vector.tensor_tensor(res[:], pairs[:, 0:n:2], pairs[:, 1:n:2], ALU.add)
+            nc.sync.dma_start(out[rows(b), first // 2 : (first + n) // 2], res[:])
+
+        def sum_on_gpsimd(b, first, n, pairs):
+            res = ring.tile([P, n // 2], F32, name="res_g", bufs=3)
+            nc.gpsimd.tensor_tensor(res[:], pairs[:, 0:n:2], pairs[:, 1:n:2], ALU.add)
+            nc.sync.dma_start(out[rows(b), first // 2 : (first + n) // 2], res[:])
+
+        plan = [[(1024, sum_on_gpsimd), (1024, sum_on_gpsimd)] for b in range(NBLK - 1)]
+        plan.append([(1024, sum_on_gpsimd), (512, sum_on_gpsimd), (256, sum_on_gpsimd), (256, sum_on_vector)])
         pending = []
-
-        def pair_sum(b, s, pairs):
-            res = ring.tile([P, PIECE // 2], F32, name="res", bufs=3)
-            nc.vector.tensor_tensor(res[:], pairs[:, 0:PIECE:2], pairs[:, 1:PIECE:2], ALU.add)
-            nc.sync.dma_start(out[P * b : P * (b + 1), s * (PIECE // 2) : (s + 1) * (PIECE // 2)], res[:])
-
         for b in range(NBLK):
-            for s in range(E // PIECE):
-                k = PIECE // 16
-                pairs = ring.tile([P, PIECE], F32, name="pairs", bufs=3)
-                nc.vector.tensor_copy(pairs[:], dm[b][:].indirect(src[:, s * k : (s + 1) * k]))
+            first = 0
+            for n, summing in plan[b]:
+                pairs = ring.tile([P, n], F32, name="pairs", bufs=4)
+                nc.vector.tensor_copy(pairs[:], dm[b][:].indirect(src[:, first // 16 : (first + n) // 16]))
                 if pending:
-                    pair_sum(*pending.pop())
-                pending.append((b, s, pairs))
-        pair_sum(*pending.pop())
+                    late = pending.pop()
+                    late[0](*late[1:])
+                pending.append((summing, b, first, n, pairs))
+                first += n
+        late = pending.pop()
+        late[0](*late[1:])

@@ -1,6 +1,7 @@
 from contextlib import ExitStack
 
 import concourse.mybir as mybir
+from concourse.masks import make_identity
 
 F32 = mybir.dt.float32
 BF16 = mybir.dt.bfloat16
@@ -19,7 +20,7 @@ PACK = 4
 CHUNK = 512
 NCHUNK = E // CHUNK
 NBLK = D // P
-PIECE = 1024
+EBLK = CHUNK // P
 
 FLOPS = 2 * DV * D * E
 
@@ -34,14 +35,16 @@ def tile_attend_gmp_sig_ew_kernel(tc, dyT, hE, ew, w_words, w_scales, offs, offs
         dst = keep.tile([P, E // 16], U16, name="dst")
         src = keep.tile([P, E // 16], U16, name="src")
         dy = [keep.tile([P, V], F32, name="dy%d" % t) for t in range(PACK)]
-        ewc = [keep.tile([P, CHUNK], F32, name="ew%d" % c) for c in range(NCHUNK)]
         h = [keep.tile([P, PACK, CHUNK], F32, name="h%d" % c) for c in range(NCHUNK)]
-        g = [keep.tile([P, PACK, CHUNK], F32, name="g%d" % c) for c in range(NCHUNK)]
-        words = keep.tile([P, 2 * D], U8, name="words", align_bytes=64)
+        held = {}
         wsc = keep.tile([P, D], U8, name="wsc", align_bytes=64)
         codes = [keep.tile([P, CHUNK], U32, name="codes%d" % c, align_bytes=64) for c in range(NCHUNK)]
         scales = [keep.tile([P, CHUNK], U8, name="scales%d" % c, align_bytes=64) for c in range(NCHUNK)]
         dm = [keep.tile([P, E], F32, name="dm%d" % b) for b in range(NBLK)]
+        ident = keep.tile([P, P], F32, name="ident")
+        ew_rows = keep.tile([P, P], F32, name="ew_rows")
+        ew_col = keep.tile([P, E // P], F32, name="ew_col")
+        ew_neg = keep.tile([P, E // P], F32, name="ew_neg")
 
         dy_planes = dyT.rearrange("(p t) v -> p t v", t=PACK)
         h_planes = hE.rearrange("(p t) e -> p t e", t=PACK)
@@ -49,49 +52,159 @@ def tile_attend_gmp_sig_ew_kernel(tc, dyT, hE, ew, w_words, w_scales, offs, offs
         def cols(c):
             return slice(c * CHUNK, (c + 1) * CHUNK)
 
+        def block(j):
+            return slice(j * P, (j + 1) * P)
+
+        make_identity(nc, ident[:])
         nc.gpsimd.memset(wsc[:].bitcast(I32), 0)
+
+        def load_h(c, t0, t1):
+            nc.sync.dma_start(h[c][:, t0:t1, :], h_planes[:, t0:t1, cols(c)])
+
+        def load_dy(t):
+            nc.sync.dma_start(dy[t][:], dy_planes[:, t, :])
+
+        def load_ew():
+            nc.sync.dma_start(ew_rows[:], ew[0:8, :].rearrange("r (j p) -> (r j) p", p=P))
+
+        ewc = {}
+
+        def load_ewc(c):
+            ewc[c] = keep.tile([P, CHUNK], F32, name="ew%d" % c)
+            nc.sync.dma_start(ewc[c][:], ew[:, cols(c)])
+
+        def reload_ewc(c):
+            ewc[c] = keep.tile([P, CHUNK], F32, name="h3")
+            nc.sync.dma_start(ewc[c][:], ew[:, cols(c)])
+
+        def load_words():
+            held["words"] = keep.tile([P, 2 * D], U8, name="v3", align_bytes=64)
+            nc.sync.dma_start(held["words"][:].bitcast(I32), w_words[0].bitcast(I32))
+
+        def load_w():
+            for q in range(4):
+                nc.sync.dma_start(
+                    wsc[32 * q : 32 * q + 4, :].bitcast(I32), w_scales[0, 4 * q : 4 * q + 4, :].bitcast(I32)
+                )
+
         nc.sync.dma_start(dst[:], offs)
-        nc.sync.dma_start(ewc[0][:], ew[:, cols(0)])
-        nc.sync.dma_start(dy[0][:], dy_planes[:, 0, :])
-        nc.sync.dma_start(ewc[1][:], ew[:, cols(1)])
-        nc.sync.dma_start(dy[1][:], dy_planes[:, 1, :])
-        nc.sync.dma_start(dy[2][:], dy_planes[:, 2, :])
-        nc.sync.dma_start(h[0][:], h_planes[:, :, cols(0)])
-        nc.sync.dma_start(dy[3][:], dy_planes[:, 3, :])
-        nc.sync.dma_start(h[1][:], h_planes[:, :, cols(1)])
-        nc.sync.dma_start(ewc[2][:], ew[:, cols(2)])
-        nc.sync.dma_start(ewc[3][:], ew[:, cols(3)])
-        nc.sync.dma_start(h[2][:], h_planes[:, :, cols(2)])
-        nc.sync.dma_start(words[:].bitcast(I32), w_words[0].bitcast(I32))
-        for q in range(4):
-            nc.sync.dma_start(
-                wsc[32 * q : 32 * q + 4, :].bitcast(I32), w_scales[0, 4 * q : 4 * q + 4, :].bitcast(I32)
-            )
-        nc.sync.dma_start(h[3][:], h_planes[:, :, cols(3)])
+        load_dy(0)
+        load_ewc(0)
+        load_ewc(1)
+        load_ew()
+        load_dy(1)
+        load_h(2, 0, 2)
+        load_dy(2)
+        load_h(2, 2, 4)
+        load_dy(3)
+        load_h(3, 0, 2)
+        load_h(3, 2, 4)
+        load_h(0, 0, 4)
+        load_h(1, 0, 4)
+        load_w()
         nc.sync.dma_start(src[:], offs2)
 
-        def gather_dy(c, t):
+        ew_turned = psum.tile([P, EBLK, P], F32, name="fwd", bufs=3)
+        nc.tensor.transpose(ew_turned[:, 0, :], ew_rows[:], ident[:])
+        nc.scalar.copy(ew_col[:], ew_turned[:, 0, 0 : E // P])
+
+        v = {}
+        u = {}
+        dz = {}
+        v_tag = ['v0', 'v1', 'v2', 'v3']
+
+        def gather_dy(c, t, factor):
+            if c not in v:
+                v[c] = keep.tile([P, PACK, CHUNK], F32, name=v_tag[c], align_bytes=64)
             k = CHUNK // 16
             nc.vector.tensor_tensor(
-                g[c][:, t, :], dy[t][:].indirect(dst[:, c * k : (c + 1) * k]), ewc[c][:], ALU.mult
+                v[c][:, t, :], dy[t][:].indirect(dst[:, c * k : (c + 1) * k]), factor, ALU.mult
             )
 
-        sq = {}
-        dz = {}
+        def slope(c, t0, t1):
+            if c not in u:
+                u[c] = keep.tile([P, PACK, CHUNK], F32, name="u%d" % c)
+            nc.scalar.activation(u[c][:, t0:t1, :], h[c][:, t0:t1, :], ACT.Square, bias=-0.5)
+            if (c, t0) in []:
+                nc.vector.tensor_scalar(u[c][:, t0:t1, :], u[c][:, t0:t1, :], -1.0, 0.25, ALU.mult, ALU.add)
+            else:
+                nc.scalar.activation(u[c][:, t0:t1, :], u[c][:, t0:t1, :], ACT.Copy, scale=-1.0, bias=0.25)
 
-        def square(c):
-            half = ring.tile([P, PACK, CHUNK], F32, name="half")
-            sq[c] = ring.tile([P, PACK, CHUNK], F32, name="sq")
-            nc.scalar.activation(half[:], h[c][:], ACT.Square, bias=-0.5)
-            nc.scalar.activation(sq[c][:], half[:], ACT.Copy, scale=-1.0, bias=0.25)
+        def new_dz(c):
+            if c not in dz:
+                dz[c] = ring.tile([P, CHUNK, PACK], BF16, name="dz%d" % c, align_bytes=64, bufs=1)
 
-        def form_dz(c):
-            dz[c] = ring.tile([P, CHUNK, PACK], BF16, name="dz", align_bytes=64)
+        rest = {}
+
+        def rest_turned(c, j):
+            fwd = psum.tile([P, PACK, P], F32, name="fwd", bufs=3)
+            for t in range(PACK):
+                nc.tensor.transpose(fwd[:, t, :], h[c][:, t, block(j)], ident[:])
+            col = slice(EBLK * c + j, EBLK * c + j + 1)
+            rest[c, j] = ring.tile([P, PACK, P], F32, name="rest", bufs=2)
+            nc.scalar.activation(rest[c, j][:], fwd[:], ACT.Identity, scale=ew_neg[:, col], bias=ew_col[:, col])
+
+        def finish_on_vector(c, j):
+            new_dz(c)
+            back = psum.tile([P, PACK, P], F32, name="back", bufs=2)
+            for t in range(PACK):
+                nc.tensor.transpose(back[:, t, :], rest[c, j][:, t, :], ident[:])
             nc.vector.tensor_tensor(
-                dz[c][:].rearrange("p (c i) t -> p c t i", i=2),
-                g[c][:].rearrange("p t (c i) -> p c t i", i=2),
-                sq[c][:].rearrange("p t (c i) -> p c t i", i=2),
+                dz[c][:, block(j), :].rearrange("p (c i) t -> p c t i", i=2),
+                back[:].rearrange("p t (c i) -> p c t i", i=2),
+                v[c][:, :, block(j)].rearrange("p t (c i) -> p c t i", i=2),
                 ALU.mult,
+            )
+
+        def finish_plain(c, half):
+            new_dz(c)
+            part = slice(half * CHUNK // 2, (half + 1) * CHUNK // 2)
+            nc.vector.tensor_tensor(
+                dz[c][:, part, :].rearrange("p (c i) t -> p c t i", i=2),
+                u[c][:, :, part].rearrange("p t (c i) -> p c t i", i=2),
+                v[c][:, :, part].rearrange("p t (c i) -> p c t i", i=2),
+                ALU.mult,
+            )
+
+        def square(c, half):
+            if c not in u:
+                u[c] = keep.tile([P, CHUNK, PACK], F32, name="u%d" % c)
+            part = slice(half * CHUNK // 2, (half + 1) * CHUNK // 2)
+            nc.scalar.activation(
+                u[c][:, part, :].rearrange("p (c i) t -> p c t i", i=2),
+                h[c][:, :, part].rearrange("p t (c i) -> p c t i", i=2),
+                ACT.Square,
+                bias=-0.5,
+            )
+
+        def finish_fused(c, half):
+            new_dz(c)
+            part = slice(half * CHUNK // 2, (half + 1) * CHUNK // 2)
+            nc.vector.scalar_tensor_tensor(
+                dz[c][:, part, :], u[c][:, part, :], 0.25, v[c][:, :, part].rearrange("p t e -> p e t"), ALU.subtract, ALU.mult
+            )
+
+        def finish_on_scalar(c, pair):
+            new_dz(c)
+            back = psum.tile([P, 2, 2, P], F32, name="back", bufs=2)
+            for m in range(2):
+                j = 2 * pair + m
+                fwd = psum.tile([P, PACK, P], F32, name="fwd", bufs=3)
+                for t in range(PACK):
+                    nc.tensor.transpose(fwd[:, t, :], v[c][:, t, block(j)], ident[:])
+                col = slice(EBLK * c + j, EBLK * c + j + 1)
+                turned = ring.tile([P, 2, P, 2], BF16, name="turned", bufs=4)
+                nc.scalar.activation(
+                    turned[:], fwd[:].rearrange("e (w i) p -> e w p i", i=2), ACT.Copy, scale=ew_col[:, col]
+                )
+                pairs_of_n = turned[:].rearrange("e w p i -> e (w p i)").bitcast(F32)
+                for w in range(2):
+                    nc.tensor.transpose(back[:, m, w, :], pairs_of_n[:, block(w)], ident[:])
+            dz_words = dz[c][:].rearrange("p e t -> p (e t)").bitcast(F32)
+            move = nc.vector.tensor_copy if (c, pair) in [] else nc.scalar.copy
+            move(
+                dz_words[:, 4 * P * pair : 4 * P * (pair + 1)].rearrange("p (m e w) -> p m e w", m=2, w=2),
+                back[:].rearrange("p m w e -> p m e w"),
             )
 
         def quantise(c):
@@ -100,76 +213,93 @@ def tile_attend_gmp_sig_ew_kernel(tc, dyT, hE, ew, w_words, w_scales, offs, offs
             )
 
         def product(b, c):
-            if b == 0:
-                acc = psum.tile([P, CHUNK], F32, name="acc_first", bufs=2)
-            else:
-                acc = psum.tile([P, CHUNK], F32, name="acc", bufs=4)
+            acc = psum.tile([P, CHUNK], F32, name="acc", bufs=3)
             nc.tensor.matmul_mx(
                 out=acc[:],
-                lhsT=words[:, 2 * P * b : 2 * P * (b + 1)].bitcast(E2M1X4),
-                lhsT_scale=wsc[:, P * b : P * (b + 1)],
+                lhsT=held["words"][:, 2 * P * b : 2 * P * (b + 1)].bitcast(E2M1X4),
+                lhsT_scale=wsc[:, block(b)],
                 rhs=codes[c][:].bitcast(E5M2X4),
                 rhs_scale=scales[c][:],
                 start=True,
                 stop=True,
             )
-            nc.scalar.copy(dm[b][:, cols(c)], acc[:])
+            if b == 0 and c in [3]:
+                nc.vector.tensor_scalar(dm[b][:, cols(c)], acc[:], [-1.0, -1.0, 1.0, 1.0][c], None, ALU.mult)
+            else:
+                nc.scalar.activation(dm[b][:, cols(c)], acc[:], ACT.Copy, scale=[-1.0, -1.0, 1.0, 1.0][c])
 
-        for t in range(PACK):
-            gather_dy(0, t)
-            gather_dy(1, t)
-        square(0)
-        square(1)
-        form_dz(0)
-        gather_dy(2, 0)
-        quantise(0)
-        product(0, 0)
-        form_dz(1)
-        gather_dy(2, 1)
-        quantise(1)
-        product(0, 1)
-        square(2)
-        gather_dy(2, 2)
-        gather_dy(2, 3)
-        form_dz(2)
-        gather_dy(3, 0)
+        gather_dy(0, 0, ewc[0][:])
+        gather_dy(1, 0, ewc[1][:])
+        gather_dy(0, 1, ewc[0][:])
+        gather_dy(1, 1, ewc[1][:])
+        gather_dy(0, 2, ewc[0][:])
+        slope(2, 0, 1)
+        gather_dy(2, 0, u[2][:, 0, :])
+        slope(2, 1, 2)
+        gather_dy(2, 1, u[2][:, 1, :])
+        gather_dy(0, 3, ewc[0][:])
+        slope(2, 2, 3)
+        gather_dy(2, 2, u[2][:, 2, :])
+        slope(2, 3, 4)
+        gather_dy(2, 3, u[2][:, 3, :])
+        slope(3, 0, 1)
+        gather_dy(3, 0, u[3][:, 0, :])
+        slope(3, 1, 2)
+        gather_dy(3, 1, u[3][:, 1, :])
+        slope(3, 2, 3)
+        gather_dy(3, 2, u[3][:, 2, :])
+        slope(3, 3, 4)
+        gather_dy(3, 3, u[3][:, 3, :])
+        reload_ewc(1)
+        gather_dy(1, 2, ewc[1][:])
+        gather_dy(1, 3, ewc[1][:])
+        finish_on_scalar(2, 0)
+        finish_on_scalar(2, 1)
+        square(0, 0)
+        square(0, 1)
+        finish_on_scalar(3, 0)
+        finish_on_scalar(3, 1)
+        load_words()
+        square(1, 0)
+        square(1, 1)
         quantise(2)
-        product(0, 2)
-        square(3)
-        for t in range(1, PACK):
-            gather_dy(3, t)
-        form_dz(3)
+        finish_fused(0, 0)
+        finish_fused(0, 1)
         quantise(3)
+        finish_fused(1, 0)
+        quantise(0)
+        finish_fused(1, 1)
+        quantise(1)
+        product(0, 2)
+        product(0, 0)
         product(0, 3)
-        for b in range(1, NBLK):
-            for c in range(NCHUNK):
-                product(b, c)
+        product(0, 1)
+        product(1, 0)
+        product(1, 1)
+        product(1, 2)
+        product(1, 3)
+        product(2, 0)
+        product(2, 1)
+        product(2, 2)
+        product(2, 3)
+        product(3, 0)
+        product(3, 1)
+        product(3, 2)
+        product(3, 3)
 
-        def rows(b):
-            return slice(P * b, P * (b + 1))
+        def pair_sum(engine, queue, tag, b, first, n, pairs):
+            res = ring.tile([P, n // 2], F32, name=tag, bufs=3)
+            engine.tensor_tensor(res[:], pairs[:, 0:n:2], pairs[:, 1:n:2], ALU.add)
+            queue.dma_start(out[block(b), first // 2 : (first + n) // 2], res[:])
 
-        def sum_on_vector(b, first, n, pairs):
-            res = ring.tile([P, n // 2], F32, name="res_v", bufs=2)
-            nc.vector.tensor_tensor(res[:], pairs[:, 0:n:2], pairs[:, 1:n:2], ALU.add)
-            nc.sync.dma_start(out[rows(b), first // 2 : (first + n) // 2], res[:])
-
-        def sum_on_gpsimd(b, first, n, pairs):
-            res = ring.tile([P, n // 2], F32, name="res_g", bufs=3)
-            nc.gpsimd.tensor_tensor(res[:], pairs[:, 0:n:2], pairs[:, 1:n:2], ALU.add)
-            nc.sync.dma_start(out[rows(b), first // 2 : (first + n) // 2], res[:])
-
-        plan = [[(1024, sum_on_gpsimd), (1024, sum_on_gpsimd)] for b in range(NBLK - 1)]
-        plan.append([(1024, sum_on_gpsimd), (512, sum_on_gpsimd), (256, sum_on_gpsimd), (256, sum_on_vector)])
-        pending = []
+        plan = [[1024, 1024] for b in range(NBLK - 1)] + [[1024, 512, 256, 256]]
         for b in range(NBLK):
             first = 0
-            for n, summing in plan[b]:
+            for n in plan[b]:
                 pairs = ring.tile([P, n], F32, name="pairs", bufs=4)
                 nc.vector.tensor_copy(pairs[:], dm[b][:].indirect(src[:, first // 16 : (first + n) // 16]))
-                if pending:
-                    late = pending.pop()
-                    late[0](*late[1:])
-                pending.append((summing, b, first, n, pairs))
+                if b == NBLK - 1 and first + n == E:
+                    pair_sum(nc.vector, nc.scalar, "res_v", b, first, n, pairs)
+                else:
+                    pair_sum(nc.gpsimd, nc.sync, "res_g", b, first, n, pairs)
                 first += n
-        late = pending.pop()
-        late[0](*late[1:])

from contextlib import ExitStack

import concourse.mybir as mybir
from concourse.masks import make_identity

F32 = mybir.dt.float32
BF16 = mybir.dt.bfloat16
U32 = mybir.dt.uint32
I32 = mybir.dt.int32
U16 = mybir.dt.uint16
U8 = mybir.dt.uint8
E5M2X4 = mybir.dt.float8_e5m2_x4
E2M1X4 = mybir.dt.float4_e2m1fn_x4
ALU = mybir.AluOpType
ACT = mybir.ActivationFunctionType

P = 128
V, E, D, DV = 1024, 2048, 512, 512
PACK = 4
CHUNK = 512
NCHUNK = E // CHUNK
NBLK = D // P
EBLK = CHUNK // P

FLOPS = 2 * DV * D * E


def tile_attend_gmp_sig_ew_kernel(tc, dyT, hE, ew, w_words, w_scales, offs, offs2, out):
    nc = tc.nc
    with ExitStack() as ctx:
        keep = ctx.enter_context(tc.tile_pool(name="keep", bufs=1))
        ring = ctx.enter_context(tc.tile_pool(name="ring", bufs=2))
        psum = ctx.enter_context(tc.psum_pool(name="psum", bufs=1))

        dst = keep.tile([P, E // 16], U16, name="dst")
        src = keep.tile([P, E // 16], U16, name="src")
        dy = [keep.tile([P, V], F32, name="dy%d" % t) for t in range(PACK)]
        h = [keep.tile([P, PACK, CHUNK], F32, name="h%d" % c) for c in range(NCHUNK)]
        held = {}
        wsc = keep.tile([P, D], U8, name="wsc", align_bytes=64)
        codes = [keep.tile([P, CHUNK], U32, name="codes%d" % c, align_bytes=64) for c in range(NCHUNK)]
        scales = [keep.tile([P, CHUNK], U8, name="scales%d" % c, align_bytes=64) for c in range(NCHUNK)]
        dm = [keep.tile([P, E], F32, name="dm%d" % b) for b in range(NBLK)]
        ident = keep.tile([P, P], F32, name="ident")
        ew_rows = keep.tile([P, P], F32, name="ew_rows")
        ew_col = keep.tile([P, E // P], F32, name="ew_col")
        ew_neg = keep.tile([P, E // P], F32, name="ew_neg")

        dy_planes = dyT.rearrange("(p t) v -> p t v", t=PACK)
        h_planes = hE.rearrange("(p t) e -> p t e", t=PACK)

        def cols(c):
            return slice(c * CHUNK, (c + 1) * CHUNK)

        def block(j):
            return slice(j * P, (j + 1) * P)

        make_identity(nc, ident[:])
        nc.gpsimd.memset(wsc[:].bitcast(I32), 0)

        def load_h(c, t0, t1):
            nc.sync.dma_start(h[c][:, t0:t1, :], h_planes[:, t0:t1, cols(c)])

        def load_dy(t):
            nc.sync.dma_start(dy[t][:], dy_planes[:, t, :])

        def load_ew():
            nc.sync.dma_start(ew_rows[:], ew[0:8, :].rearrange("r (j p) -> (r j) p", p=P))

        ewc = {}

        def load_ewc(c):
            ewc[c] = keep.tile([P, CHUNK], F32, name="ew%d" % c)
            nc.sync.dma_start(ewc[c][:], ew[:, cols(c)])

        def reload_ewc(c):
            ewc[c] = keep.tile([P, CHUNK], F32, name="h3")
            nc.sync.dma_start(ewc[c][:], ew[:, cols(c)])

        def load_words():
            held["words"] = keep.tile([P, 2 * D], U8, name="v3", align_bytes=64)
            nc.sync.dma_start(held["words"][:].bitcast(I32), w_words[0].bitcast(I32))

        def load_w():
            for q in range(4):
                nc.sync.dma_start(
                    wsc[32 * q : 32 * q + 4, :].bitcast(I32), w_scales[0, 4 * q : 4 * q + 4, :].bitcast(I32)
                )

        nc.sync.dma_start(dst[:], offs)
        load_dy(0)
        load_ewc(0)
        load_ewc(1)
        load_ew()
        load_dy(1)
        load_h(2, 0, 2)
        load_dy(2)
        load_h(2, 2, 4)
        load_dy(3)
        load_h(3, 0, 2)
        load_h(3, 2, 4)
        load_h(0, 0, 4)
        load_h(1, 0, 4)
        load_w()
        nc.sync.dma_start(src[:], offs2)

        ew_turned = psum.tile([P, EBLK, P], F32, name="fwd", bufs=3)
        nc.tensor.transpose(ew_turned[:, 0, :], ew_rows[:], ident[:])
        nc.scalar.copy(ew_col[:], ew_turned[:, 0, 0 : E // P])

        v = {}
        u = {}
        dz = {}
        v_tag = ['v0', 'v1', 'v2', 'v3']

        def gather_dy(c, t, factor):
            if c not in v:
                v[c] = keep.tile([P, PACK, CHUNK], F32, name=v_tag[c], align_bytes=64)
            k = CHUNK // 16
            nc.vector.tensor_tensor(
                v[c][:, t, :], dy[t][:].indirect(dst[:, c * k : (c + 1) * k]), factor, ALU.mult
            )

        def slope(c, t0, t1):
            if c not in u:
                u[c] = keep.tile([P, PACK, CHUNK], F32, name="u%d" % c)
            nc.scalar.activation(u[c][:, t0:t1, :], h[c][:, t0:t1, :], ACT.Square, bias=-0.5)
            if (c, t0) in []:
                nc.vector.tensor_scalar(u[c][:, t0:t1, :], u[c][:, t0:t1, :], -1.0, 0.25, ALU.mult, ALU.add)
            else:
                nc.scalar.activation(u[c][:, t0:t1, :], u[c][:, t0:t1, :], ACT.Copy, scale=-1.0, bias=0.25)

        def new_dz(c):
            if c not in dz:
                dz[c] = ring.tile([P, CHUNK, PACK], BF16, name="dz%d" % c, align_bytes=64, bufs=1)

        rest = {}

        def rest_turned(c, j):
            fwd = psum.tile([P, PACK, P], F32, name="fwd", bufs=3)
            for t in range(PACK):
                nc.tensor.transpose(fwd[:, t, :], h[c][:, t, block(j)], ident[:])
            col = slice(EBLK * c + j, EBLK * c + j + 1)
            rest[c, j] = ring.tile([P, PACK, P], F32, name="rest", bufs=2)
            nc.scalar.activation(rest[c, j][:], fwd[:], ACT.Identity, scale=ew_neg[:, col], bias=ew_col[:, col])

        def finish_on_vector(c, j):
            new_dz(c)
            back = psum.tile([P, PACK, P], F32, name="back", bufs=2)
            for t in range(PACK):
                nc.tensor.transpose(back[:, t, :], rest[c, j][:, t, :], ident[:])
            nc.vector.tensor_tensor(
                dz[c][:, block(j), :].rearrange("p (c i) t -> p c t i", i=2),
                back[:].rearrange("p t (c i) -> p c t i", i=2),
                v[c][:, :, block(j)].rearrange("p t (c i) -> p c t i", i=2),
                ALU.mult,
            )

        def finish_plain(c, half):
            new_dz(c)
            part = slice(half * CHUNK // 2, (half + 1) * CHUNK // 2)
            nc.vector.tensor_tensor(
                dz[c][:, part, :].rearrange("p (c i) t -> p c t i", i=2),
                u[c][:, :, part].rearrange("p t (c i) -> p c t i", i=2),
                v[c][:, :, part].rearrange("p t (c i) -> p c t i", i=2),
                ALU.mult,
            )

        def square(c, half):
            if c not in u:
                u[c] = keep.tile([P, CHUNK, PACK], F32, name="u%d" % c)
            part = slice(half * CHUNK // 2, (half + 1) * CHUNK // 2)
            nc.scalar.activation(
                u[c][:, part, :].rearrange("p (c i) t -> p c t i", i=2),
                h[c][:, :, part].rearrange("p t (c i) -> p c t i", i=2),
                ACT.Square,
                bias=-0.5,
            )

        def finish_fused(c, half):
            new_dz(c)
            part = slice(half * CHUNK // 2, (half + 1) * CHUNK // 2)
            nc.vector.scalar_tensor_tensor(
                dz[c][:, part, :], u[c][:, part, :], 0.25, v[c][:, :, part].rearrange("p t e -> p e t"), ALU.subtract, ALU.mult
            )

        def finish_on_scalar(c, pair):
            new_dz(c)
            back = psum.tile([P, 2, 2, P], F32, name="back", bufs=2)
            for m in range(2):
                j = 2 * pair + m
                fwd = psum.tile([P, PACK, P], F32, name="fwd", bufs=3)
                for t in range(PACK):
                    nc.tensor.transpose(fwd[:, t, :], v[c][:, t, block(j)], ident[:])
                col = slice(EBLK * c + j, EBLK * c + j + 1)
                turned = ring.tile([P, 2, P, 2], BF16, name="turned", bufs=4)
                nc.scalar.activation(
                    turned[:], fwd[:].rearrange("e (w i) p -> e w p i", i=2), ACT.Copy, scale=ew_col[:, col]
                )
                pairs_of_n = turned[:].rearrange("e w p i -> e (w p i)").bitcast(F32)
                for w in range(2):
                    nc.tensor.transpose(back[:, m, w, :], pairs_of_n[:, block(w)], ident[:])
            dz_words = dz[c][:].rearrange("p e t -> p (e t)").bitcast(F32)
            move = nc.vector.tensor_copy if (c, pair) in [] else nc.scalar.copy
            move(
                dz_words[:, 4 * P * pair : 4 * P * (pair + 1)].rearrange("p (m e w) -> p m e w", m=2, w=2),
                back[:].rearrange("p m w e -> p m e w"),
            )

        def quantise(c):
            nc.vector.quantize_mx(
                out=codes[c][:].bitcast(E5M2X4), scales=scales[c][:], in_=dz[c][:].rearrange("p e t -> p (e t)")
            )

        def product(b, c):
            acc = psum.tile([P, CHUNK], F32, name="acc", bufs=3)
            nc.tensor.matmul_mx(
                out=acc[:],
                lhsT=held["words"][:, 2 * P * b : 2 * P * (b + 1)].bitcast(E2M1X4),
                lhsT_scale=wsc[:, block(b)],
                rhs=codes[c][:].bitcast(E5M2X4),
                rhs_scale=scales[c][:],
                start=True,
                stop=True,
            )
            if b == 0 and c in [3]:
                nc.vector.tensor_scalar(dm[b][:, cols(c)], acc[:], [-1.0, -1.0, 1.0, 1.0][c], None, ALU.mult)
            else:
                nc.scalar.activation(dm[b][:, cols(c)], acc[:], ACT.Copy, scale=[-1.0, -1.0, 1.0, 1.0][c])

        gather_dy(0, 0, ewc[0][:])
        gather_dy(1, 0, ewc[1][:])
        gather_dy(0, 1, ewc[0][:])
        gather_dy(1, 1, ewc[1][:])
        gather_dy(0, 2, ewc[0][:])
        slope(2, 0, 1)
        gather_dy(2, 0, u[2][:, 0, :])
        slope(2, 1, 2)
        gather_dy(2, 1, u[2][:, 1, :])
        gather_dy(0, 3, ewc[0][:])
        slope(2, 2, 3)
        gather_dy(2, 2, u[2][:, 2, :])
        slope(2, 3, 4)
        gather_dy(2, 3, u[2][:, 3, :])
        slope(3, 0, 1)
        gather_dy(3, 0, u[3][:, 0, :])
        slope(3, 1, 2)
        gather_dy(3, 1, u[3][:, 1, :])
        slope(3, 2, 3)
        gather_dy(3, 2, u[3][:, 2, :])
        slope(3, 3, 4)
        gather_dy(3, 3, u[3][:, 3, :])
        reload_ewc(1)
        gather_dy(1, 2, ewc[1][:])
        gather_dy(1, 3, ewc[1][:])
        finish_on_scalar(2, 0)
        finish_on_scalar(2, 1)
        square(0, 0)
        square(0, 1)
        finish_on_scalar(3, 0)
        finish_on_scalar(3, 1)
        load_words()
        square(1, 0)
        square(1, 1)
        quantise(2)
        finish_fused(0, 0)
        finish_fused(0, 1)
        quantise(3)
        finish_fused(1, 0)
        quantise(0)
        finish_fused(1, 1)
        quantise(1)
        product(0, 2)
        product(0, 0)
        product(0, 3)
        product(0, 1)
        product(1, 0)
        product(1, 1)
        product(1, 2)
        product(1, 3)
        product(2, 0)
        product(2, 1)
        product(2, 2)
        product(2, 3)
        product(3, 0)
        product(3, 1)
        product(3, 2)
        product(3, 3)

        def pair_sum(engine, queue, tag, b, first, n, pairs):
            res = ring.tile([P, n // 2], F32, name=tag, bufs=3)
            engine.tensor_tensor(res[:], pairs[:, 0:n:2], pairs[:, 1:n:2], ALU.add)
            queue.dma_start(out[block(b), first // 2 : (first + n) // 2], res[:])

        plan = [[1024, 1024] for b in range(NBLK - 1)] + [[1024, 512, 256, 256]]
        for b in range(NBLK):
            first = 0
            for n in plan[b]:
                pairs = ring.tile([P, n], F32, name="pairs", bufs=4)
                nc.vector.tensor_copy(pairs[:], dm[b][:].indirect(src[:, first // 16 : (first + n) // 16]))
                if b == NBLK - 1 and first + n == E:
                    pair_sum(nc.vector, nc.scalar, "res_v", b, first, n, pairs)
                else:
                    pair_sum(nc.gpsimd, nc.sync, "res_g", b, first, n, pairs)
                first += n
